import numpy as np
import ml_dtypes


def mxq(x, axis, fmt="e4m3"):
    dtype, down = {"e4m3": (ml_dtypes.float8_e4m3fn, 7), "e5m2": (ml_dtypes.float8_e5m2, 14)}[fmt]
    v = np.moveaxis(np.asarray(x, np.float32).astype(ml_dtypes.bfloat16).astype(np.float64), axis, -1)
    blocks = v.reshape(v.shape[:-1] + (-1, 32))
    amax = np.abs(blocks).max(-1, keepdims=True)
    byte = np.maximum(np.where(amax > 0, np.frexp(amax)[1] - 1 + 127, 0) - down, 1)
    scale = np.exp2(byte - 127.0)
    codes = (blocks / scale).astype(np.float32).astype(dtype).astype(np.float64)
    return np.moveaxis((codes * scale).reshape(v.shape), -1, axis)


WIDE = False


def mx_kscale(k):
    if not WIDE:
        return np.ones(k)
    levels = np.array([10, -10, 5, -5, 0])
    if k % 512:
        return np.exp2(np.random.permutation(np.resize(levels, k // 32))).repeat(32)
    a = np.empty((k // 512, 16))
    for p in range(k // 512):
        a[p, :8] = np.random.permutation(np.resize(levels, 8))
        for g in range(8):
            far = levels[np.abs(levels - a[p, g]) >= 10]
            a[p, g + 8] = far[np.random.randint(len(far))]
    return np.exp2(a.ravel()).repeat(32)


def f64(x):
    return np.asarray(x).astype(np.float64)


def striped(idx):
    return np.tile(np.asarray(idx).reshape(-1, 16).T, (8, 1)).astype(np.uint16)


def unstriped(offs):
    return offs[:16].T.reshape(-1).astype(np.int64)


E2M1 = np.array([0.0, 0.5, 1.0, 1.5, 2.0, 3.0, 4.0, 6.0, -0.0, -0.5, -1.0, -1.5, -2.0, -3.0, -4.0, -6.0])


def pack_weight(w, fmt):
    k, n = w.shape
    w = f64(np.asarray(w, np.float32).astype(ml_dtypes.bfloat16)).reshape(k // 32, 32, n)
    amax = np.abs(w).max(1)
    if fmt == "e4m3":
        byte = np.frexp(amax)[1] - 1 + 127 - 7
    else:
        mant, ex = np.frexp(amax / 6.0)
        byte = np.where(mant > 0.5, ex, ex - 1) + 127
    byte = np.clip(np.where(amax > 0, byte, 1), 1, 254)
    scaled = (w * np.exp2(127.0 - byte)[:, None, :]).reshape(k, n).astype(np.float32)
    by_word = np.ascontiguousarray(scaled.reshape(k // 512, 128, 4, n).transpose(0, 1, 3, 2))
    if fmt == "e4m3":
        words = by_word.astype(ml_dtypes.float8_e4m3fn).view(np.uint8)
    else:
        c = by_word.astype(ml_dtypes.float4_e2m1fn).view(np.uint8) & 0xF
        words = (c[..., 0::2] | (c[..., 1::2] << 4)).reshape(k // 512, 128, 2 * n)
    return np.ascontiguousarray(words), np.ascontiguousarray(byte.astype(np.uint8).reshape(k // 512, 16, n))


def unpack_weight(words, scales, fmt):
    g, _, n = scales.shape
    words = np.ascontiguousarray(words).reshape(g, 128, n, -1)
    if fmt == "e4m3":
        vals = words.view(ml_dtypes.float8_e4m3fn).astype(np.float64)
    else:
        nib = np.empty((g, 128, n, 4), np.uint8)
        nib[..., 0::2] = words & 0xF
        nib[..., 1::2] = words >> 4
        vals = E2M1[nib]
    vals = vals * np.repeat(np.exp2(scales.astype(np.float64) - 127.0), 8, axis=1)[..., None]
    return vals.transpose(0, 1, 3, 2).reshape(g * 512, n)


def bf(x):
    return np.asarray(x, np.float32).astype(ml_dtypes.bfloat16)


def planes(Y):
    r, m = Y.shape
    b = f64(bf(Y)).reshape(r // 32, 32, m)
    amax = np.abs(b).max(1)
    byte = np.clip(np.where(amax > 0, np.frexp(amax)[1] - 1 + 127 - 7, 1), 1, 254)
    codes = (b * np.exp2(127.0 - byte)[:, None, :]).reshape(r, m).astype(np.float32).astype(ml_dtypes.float8_e4m3fn).view(np.uint8)
    words = codes.reshape(r // 512, 128, 4, m).transpose(0, 1, 3, 2)
    return np.ascontiguousarray(words), np.ascontiguousarray(byte.astype(np.uint8).reshape(r // 512, 16, m))


K, T, J, B, L, N = 512, 2048, 1024, 128, 512, 512


def setup_inputs():
    n = np.random.standard_normal
    idx = np.random.permutation(T)[:J]
    fk = mx_kscale(K)
    fl = mx_kscale(L)
    wap = pack_weight(n((K, N)) * 1 / np.sqrt(K) / fk[:, None], "e4m3")
    wbp = pack_weight(n((K, N)) * 1 / np.sqrt(K) / fk[:, None], "e2m1")
    gqp = pack_weight(n((L, B)) / fl[:, None], "e2m1")
    return {
        "xt": (n((K, T))).astype(np.float32),
        "fa": (np.random.uniform(0.5, 2.0, (K, 1)) * fk[:, None]).astype(np.float32),
        "fb": (np.random.uniform(0.5, 2.0, (K, 1)) * fk[:, None]).astype(np.float32),
        "wa_words": wap[0],
        "wa_scales": wap[1],
        "wb_words": wbp[0],
        "wb_scales": wbp[1],
        "gq_words": gqp[0],
        "gq_scales": gqp[1],
        "wc": (n((L, N)) * 1 / np.sqrt(L) * fl[:, None]).astype(np.float32),
        "offs": striped(idx),
    }


def reference(xt, fa, fb, wa_words, wa_scales, wb_words, wb_scales, gq_words, gq_scales, wc, offs):
    idx = unstriped(offs)
    wau = unpack_weight(wa_words, wa_scales, "e4m3")
    wbu = unpack_weight(wb_words, wb_scales, "e2m1")
    gqu = unpack_weight(gq_words, gq_scales, "e2m1")
    u = f64(xt)[:, idx].reshape(K, B, J // B).max(axis=2) * f64(fa)
    v = f64(xt)[:, idx].reshape(K, B, J // B).mean(axis=2) * f64(fb)
    uq = mxq(u, 0, "e4m3")
    vq = mxq(v, 0, "e4m3")
    wcq = mxq(f64(wc), 0, "e4m3")
    y = wau.T @ uq + wbu.T @ vq + wcq.T @ gqu
    words, scales = planes(y)
    return y, words, scales

@@ -1,0 +1,202 @@
+from contextlib import ExitStack
+
+import concourse.mybir as mybir
+from concourse.masks import make_identity
+
+K, T, J, B, L, N = 512, 2048, 1024, 128, 512, 512
+FLOPS = 3 * 2 * K * N * B
+
+F32 = mybir.dt.float32
+BF16 = mybir.dt.bfloat16
+I32 = mybir.dt.int32
+U32 = mybir.dt.uint32
+U16 = mybir.dt.uint16
+U8 = mybir.dt.uint8
+FP8X4 = mybir.dt.float8_e4m3fn_x4
+FP4X4 = mybir.dt.float4_e2m1fn_x4
+MAX = mybir.AluOpType.max
+COPY = mybir.ActivationFunctionType.Copy
+
+P = 128
+PACK = 4
+GROUP = J // B
+QUADS = 4
+
+
+def tile_list_group_range_pooling_pl_kernel(
+    tc, xt, fa, fb, wa_words, wa_scales, wb_words, wb_scales, gq_words, gq_scales, wc, offs, out_0, out_1, out_2
+):
+    nc = tc.nc
+    with ExitStack() as ctx:
+        keep = ctx.enter_context(tc.tile_pool(name="keep", bufs=1))
+        ring = ctx.enter_context(tc.tile_pool(name="ring", bufs=2))
+        ps_sum = ctx.enter_context(tc.psum_pool(name="ps_sum", bufs=3))
+        ps_back = ctx.enter_context(tc.psum_pool(name="ps_back", bufs=3))
+        ps_y = ctx.enter_context(tc.psum_pool(name="ps_y", bufs=1))
+
+        offsets = keep.tile([P, J // 16], U16, name="offsets")
+        window = [keep.tile([P, T], F32, name="window%d" % t, align_bytes=64) for t in range(PACK)]
+        x_planes = xt.rearrange("(p t) c -> t p c", t=PACK)
+        wc_rows = wc.rearrange("(p j) n -> p j n", j=PACK)
+        half = N // 2
+        wc_raw = [keep.tile([P, PACK, half], F32, name="wc_raw%d" % h, align_bytes=64) for h in range(2)]
+        wa_raw = keep.tile([P, N], U32, name="wa_raw", align_bytes=64)
+        wb_raw = keep.tile([P, 2 * N], U8, name="wb_raw", align_bytes=64)
+        gq_codes = keep.tile([P, 2 * B], U8, name="gq_codes", align_bytes=64)
+        fa_sb = keep.tile([P, PACK], F32, name="fa_sb")
+        fb_sb = keep.tile([P, PACK], F32, name="fb_sb")
+        sb_tile = keep.tile([P, N], U8, name="sb_raw", align_bytes=64)
+        given = keep.tile([P, N + B], U8, name="given_scales", align_bytes=64)
+        sa_raw, sb_raw, gq_scale = given[:, 0:N], sb_tile[:], given[:, N : N + B]
+
+        def load_scale_rows(queue, dst, src):
+            for q in range(QUADS):
+                queue.dma_start(out=dst[32 * q : 32 * q + 4, :].bitcast(I32), in_=src[0, 4 * q : 4 * q + 4, :].bitcast(I32))
+
+        nc.vector.memset(sb_raw.bitcast(I32), 0)
+        nc.vector.memset(given[:].bitcast(I32), 0)
+
+        nc.sync.dma_start(offsets[:], offs)
+        nc.sync.dma_start(out=window[0][:], in_=x_planes[0])
+        nc.scalar.dma_start(out=wb_raw[:].bitcast(I32), in_=wb_words[0].bitcast(I32))
+        nc.scalar.dma_start(out=fb_sb[:], in_=fb.rearrange("(p t) o -> p (t o)", t=PACK))
+        nc.scalar.dma_start(out=fa_sb[:], in_=fa.rearrange("(p t) o -> p (t o)", t=PACK))
+        for t in range(1, PACK):
+            nc.sync.dma_start(out=window[t][:], in_=x_planes[t])
+        nc.sync.dma_start(out=wc_raw[0][:], in_=wc_rows[:, :, 0:half])
+        nc.sync.dma_start(out=wc_raw[1][:], in_=wc_rows[:, :, half:N])
+        nc.sync.dma_start(out=wa_raw[:].bitcast(I32), in_=wa_words[0].rearrange("p n r -> p (n r)").bitcast(I32))
+        nc.sync.dma_start(out=gq_codes[:].bitcast(I32), in_=gq_words[0].bitcast(I32))
+        load_scale_rows(nc.sync, sa_raw, wa_scales)
+
+        ident = keep.tile([P, P], F32, name="ident", align_bytes=64)
+        make_identity(nc, ident[:])
+        load_scale_rows(nc.gpsimd, sb_raw, wb_scales)
+        load_scale_rows(nc.gpsimd, gq_scale, gq_scales)
+
+        wb_codes = keep.tile([P, 2 * N], U8, name="wb_codes", align_bytes=64)
+        nc.vector.tensor_copy(
+            out=wb_codes[:].rearrange("p (s m e) -> p s m e", s=PACK, e=2),
+            in_=wb_raw[:].rearrange("p (m s e) -> p s m e", s=PACK, e=2),
+        )
+
+        def deal(dealt, raw):
+            nc.vector.tensor_copy(out=dealt.rearrange("p (s m) -> p s m", s=PACK), in_=raw.rearrange("p (m s) -> p s m", s=PACK))
+
+        picked_all = keep.tile([P, PACK * J], F32, name="picked_all", align_bytes=64)
+        picked = [picked_all[:, t * J : (t + 1) * J] for t in range(PACK)]
+        u_in = keep.tile([P, B * PACK], BF16, name="u_in", align_bytes=64)
+        v_in = keep.tile([P, B * PACK], BF16, name="v_in", align_bytes=64)
+
+        def mean_of_plane(t):
+            sums = ps_sum.tile([P, P], F32, name="sums")
+            for r in range(GROUP):
+                nc.tensor.matmul(
+                    sums[:], lhsT=picked[t][:, r:J:GROUP], rhs=ident[:], is_transpose=True, start=(r == 0), stop=(r == GROUP - 1)
+                )
+            if t == 2:
+                means = keep.tile([P, P], F32, name="means_late", tag="wc_raw1", align_bytes=64)
+            else:
+                means = ring.tile([P, P], F32, name="means", align_bytes=64)
+            nc.scalar.activation(out=means[:], in_=sums[:], func=COPY, scale=1.0 / GROUP)
+            back = ps_back.tile([P, P], F32, name="back")
+            nc.tensor.transpose(back[:], means[:], ident[:])
+            nc.scalar.activation(out=v_in[:, t : B * PACK : PACK], in_=back[:], func=COPY, scale=fb_sb[:, t : t + 1])
+
+        def halve(dst, src, width):
+            pairs = src.rearrange("p (g h i) -> p g h i", h=2, i=width)
+            nc.vector.tensor_tensor(dst.rearrange("p (g i) -> p g i", i=width), pairs[:, :, 0, :], pairs[:, :, 1, :], MAX)
+
+        fours_all = keep.tile([P, PACK * J // 2], F32, name="fours_all", align_bytes=64)
+        fours = [fours_all[:, t * J // 2 : (t + 1) * J // 2] for t in range(PACK)]
+        twos = [keep.tile([P, J // 4], F32, name="twos%d" % t, align_bytes=64) for t in range(PACK)]
+        tops = [keep.tile([P, B], F32, name="tops%d" % t, align_bytes=64) for t in range(PACK)]
+
+        def finish_max(t):
+            halve(tops[t][:], twos[t][:], 1)
+            nc.scalar.activation(out=u_in[:, t : B * PACK : PACK], in_=tops[t][:], func=COPY, scale=fa_sb[:, t : t + 1])
+
+        wc_in = keep.tile([P, N * PACK], BF16, name="wc_in", align_bytes=64)
+        wc_view = wc_in[:].rearrange("p (s m j) -> p m s j", s=PACK, j=PACK)
+
+        def cast_wc(h):
+            ms = half // PACK
+            nc.scalar.copy(
+                out=wc_view[:, h * ms : (h + 1) * ms, :, :], in_=wc_raw[h][:].rearrange("p j (m s) -> p m s j", s=PACK)
+            )
+
+        for t in range(PACK):
+            nc.vector.tensor_copy(picked[t], window[t][:].indirect(offsets[:]))
+            if t == 2:
+                cast_wc(0)
+                cast_wc(1)
+            mean_of_plane(t)
+
+        wc_codes = keep.tile([P, N], U32, name="wc_codes", align_bytes=64)
+        wc_scale = keep.tile([P, N], U8, name="wc_scale", align_bytes=64)
+        halve(fours_all[:], picked_all[:], 4)
+        nc.vector.quantize_mx(out=wc_codes[:].bitcast(FP8X4), scales=wc_scale[:], in_=wc_in[:])
+        halve(twos[0][:], fours[0], 2)
+        halve(twos[1][:], fours[1], 2)
+        finish_max(0)
+        halve(twos[2][:], fours[2], 2)
+        finish_max(1)
+        wb_scale = keep.tile([P, N], U8, name="wb_scale", tag="twos0", align_bytes=64)
+        deal(wb_scale[:], sb_raw)
+        halve(twos[3][:], fours[3], 2)
+        finish_max(2)
+        finish_max(3)
+
+        u_codes = keep.tile([P, B], U32, name="u_codes", align_bytes=64)
+        u_scale = keep.tile([P, B], U8, name="u_scale", align_bytes=64)
+        v_codes = keep.tile([P, B], U32, name="v_codes", align_bytes=64)
+        v_scale = keep.tile([P, B], U8, name="v_scale", align_bytes=64)
+        nc.vector.quantize_mx(out=v_codes[:].bitcast(FP8X4), scales=v_scale[:], in_=v_in[:])
+        wa_codes = keep.tile([P, N], U32, name="wa_codes", tag="fours_all", align_bytes=64)
+        wa_scale = keep.tile([P, N], U8, name="wa_scale", tag="twos2", align_bytes=64)
+        deal(wa_codes[:].bitcast(I32), wa_raw[:].bitcast(I32))
+        deal(wa_scale[:], sa_raw)
+        nc.vector.quantize_mx(out=u_codes[:].bitcast(FP8X4), scales=u_scale[:], in_=u_in[:])
+
+        banks = [ps_y.tile([P, 2, B], F32, name="y_bank%d" % h) for h in range(2)]
+        for term in range(3):
+            for s in range(PACK):
+                cols = slice(s * P, (s + 1) * P)
+                if term == 0:
+                    lhs, lhs_scale = wc_codes[:, cols].bitcast(FP8X4), wc_scale[:, cols]
+                    rhs, rhs_scale = gq_codes[:].bitcast(FP4X4), gq_scale
+                elif term == 1:
+                    lhs, lhs_scale = wb_codes[:, 2 * s * P : 2 * (s + 1) * P].bitcast(FP4X4), wb_scale[:, cols]
+                    rhs, rhs_scale = v_codes[:].bitcast(FP8X4), v_scale[:]
+                else:
+                    lhs, lhs_scale = wa_codes[:, cols].bitcast(FP8X4), wa_scale[:, cols]
+                    rhs, rhs_scale = u_codes[:].bitcast(FP8X4), u_scale[:]
+                nc.tensor.matmul_mx(
+                    out=banks[s // 2][:, s % 2, :],
+                    lhsT=lhs,
+                    lhsT_scale=lhs_scale,
+                    rhs=rhs,
+                    rhs_scale=rhs_scale,
+                    start=(term == 0 and s % 2 == 0),
+                    stop=(term == 2 and s % 2 == 1),
+                )
+
+        y_sb = keep.tile([P, PACK * B], F32, name="y_sb", align_bytes=64)
+        y_rows = out_0.rearrange("(p s) b -> p (s b)", s=PACK)
+        nc.scalar.copy(out=y_sb[:, 0 : 2 * B], in_=banks[0][:].rearrange("p s b -> p (s b)"))
+        nc.vector.tensor_copy(out=y_sb[:, 2 * B : 4 * B], in_=banks[1][:].rearrange("p s b -> p (s b)"))
+        nc.sync.dma_start(out=y_rows[:, 0 : 2 * B], in_=y_sb[:, 0 : 2 * B])
+        nc.sync.dma_start(out=y_rows[:, 2 * B : 4 * B], in_=y_sb[:, 2 * B : 4 * B])
+
+        y_in = keep.tile([P, B * PACK], BF16, name="y_in", align_bytes=64)
+        y_codes = keep.tile([P, B], U32, name="y_codes", align_bytes=64)
+        y_scale = keep.tile([P, B], U8, name="y_scale", align_bytes=64)
+        nc.vector.tensor_copy(
+            out=y_in[:].rearrange("p (c i s) -> p c s i", i=4, s=PACK),
+            in_=y_sb[:].rearrange("p (s c i) -> p c s i", s=PACK, i=4),
+        )
+        nc.vector.quantize_mx(out=y_codes[:].bitcast(FP8X4), scales=y_scale[:], in_=y_in[:])
+        nc.sync.dma_start(out=out_1[0].rearrange("p c r -> p (c r)").bitcast(I32), in_=y_codes[:].bitcast(I32))
+        for q in range(QUADS):
+            queue = nc.scalar if q % 2 == 0 else nc.sync
+            queue.dma_start(out=out_2[0, 4 * q : 4 * q + 4, :].bitcast(I32), in_=y_scale[32 * q : 32 * q + 4, :].bitcast(I32))

@@ -15,6 +15,7 @@ U8 = mybir.dt.uint8
 FP8X4 = mybir.dt.float8_e4m3fn_x4
 FP4X4 = mybir.dt.float4_e2m1fn_x4
 MAX = mybir.AluOpType.max
+MULT = mybir.AluOpType.mult
 COPY = mybir.ActivationFunctionType.Copy
 
 P = 128
@@ -29,7 +30,6 @@ def tile_list_group_range_pooling_pl_kernel(
     nc = tc.nc
     with ExitStack() as ctx:
         keep = ctx.enter_context(tc.tile_pool(name="keep", bufs=1))
-        ring = ctx.enter_context(tc.tile_pool(name="ring", bufs=2))
         ps_sum = ctx.enter_context(tc.psum_pool(name="ps_sum", bufs=3))
         ps_back = ctx.enter_context(tc.psum_pool(name="ps_back", bufs=3))
         ps_y = ctx.enter_context(tc.psum_pool(name="ps_y", bufs=1))
@@ -76,45 +76,44 @@ def tile_list_group_range_pooling_pl_kernel(
 
         wb_codes = keep.tile([P, 2 * N], U8, name="wb_codes", align_bytes=64)
         nc.vector.tensor_copy(
-            out=wb_codes[:].rearrange("p (s m e) -> p s m e", s=PACK, e=2),
-            in_=wb_raw[:].rearrange("p (m s e) -> p s m e", s=PACK, e=2),
+            out=wb_codes[:].rearrange("p (s m e) -> p m s e", s=PACK, e=2),
+            in_=wb_raw[:].rearrange("p (m s e) -> p m s e", s=PACK, e=2),
         )
 
         def deal(dealt, raw):
-            nc.vector.tensor_copy(out=dealt.rearrange("p (s m) -> p s m", s=PACK), in_=raw.rearrange("p (m s) -> p s m", s=PACK))
+            nc.vector.tensor_copy(out=dealt.rearrange("p (s m) -> p m s", s=PACK), in_=raw.rearrange("p (m s) -> p m s", s=PACK))
 
         picked_all = keep.tile([P, PACK * J], F32, name="picked_all", align_bytes=64)
         picked = [picked_all[:, t * J : (t + 1) * J] for t in range(PACK)]
         u_in = keep.tile([P, B * PACK], BF16, name="u_in", align_bytes=64)
         v_in = keep.tile([P, B * PACK], BF16, name="v_in", align_bytes=64)
 
-        def mean_of_plane(t):
-            sums = ps_sum.tile([P, P], F32, name="sums")
-            for r in range(GROUP):
-                nc.tensor.matmul(
-                    sums[:], lhsT=picked[t][:, r:J:GROUP], rhs=ident[:], is_transpose=True, start=(r == 0), stop=(r == GROUP - 1)
-                )
-            if t == 2:
-                means = keep.tile([P, P], F32, name="means_late", tag="wc_raw1", align_bytes=64)
-            else:
-                means = ring.tile([P, P], F32, name="means", align_bytes=64)
+        def means_of_planes(planes, tag):
+            sums = ps_sum.tile([P, len(planes) * P], F32, name="sums")
+            for n, t in enumerate(planes):
+                for r in range(GROUP):
+                    nc.tensor.matmul(
+                        sums[:, n * P : (n + 1) * P],
+                        lhsT=picked[t][:, r:J:GROUP],
+                        rhs=ident[:],
+                        is_transpose=True,
+                        start=(r == 0),
+                        stop=(r == GROUP - 1),
+                    )
+            means = keep.tile([P, len(planes) * P], F32, name="means", tag=tag, align_bytes=64)
             nc.scalar.activation(out=means[:], in_=sums[:], func=COPY, scale=1.0 / GROUP)
-            back = ps_back.tile([P, P], F32, name="back")
-            nc.tensor.transpose(back[:], means[:], ident[:])
-            nc.scalar.activation(out=v_in[:, t : B * PACK : PACK], in_=back[:], func=COPY, scale=fb_sb[:, t : t + 1])
+            for n, t in enumerate(planes):
+                back = ps_back.tile([P, P], F32, name="back")
+                nc.tensor.transpose(back[:], means[:, n * P : (n + 1) * P], ident[:])
+                nc.scalar.activation(out=v_in[:, t : B * PACK : PACK], in_=back[:], func=COPY, scale=fb_sb[:, t : t + 1])
 
         def halve(dst, src, width):
             pairs = src.rearrange("p (g h i) -> p g h i", h=2, i=width)
             nc.vector.tensor_tensor(dst.rearrange("p (g i) -> p g i", i=width), pairs[:, :, 0, :], pairs[:, :, 1, :], MAX)
 
-        fours_all = keep.tile([P, PACK * J // 2], F32, name="fours_all", align_bytes=64)
-        fours = [fours_all[:, t * J // 2 : (t + 1) * J // 2] for t in range(PACK)]
-        twos = [keep.tile([P, J // 4], F32, name="twos%d" % t, align_bytes=64) for t in range(PACK)]
-        tops = [keep.tile([P, B], F32, name="tops%d" % t, align_bytes=64) for t in range(PACK)]
-
-        def finish_max(t):
-            halve(tops[t][:], twos[t][:], 1)
-            nc.scalar.activation(out=u_in[:, t : B * PACK : PACK], in_=tops[t][:], func=COPY, scale=fa_sb[:, t : t + 1])
+        fours = keep.tile([P, PACK * J // 2], F32, name="fours", align_bytes=64)
+        twos = keep.tile([P, PACK * J // 4], F32, name="twos", align_bytes=64)
+        tops = keep.tile([P, PACK * B], F32, name="tops", align_bytes=64)
 
         wc_in = keep.tile([P, N * PACK], BF16, name="wc_in", align_bytes=64)
         wc_view = wc_in[:].rearrange("p (s m j) -> p m s j", s=PACK, j=PACK)
@@ -127,34 +126,37 @@ def tile_list_group_range_pooling_pl_kernel(
 
         for t in range(PACK):
             nc.vector.tensor_copy(picked[t], window[t][:].indirect(offsets[:]))
-            if t == 2:
-                cast_wc(0)
-                cast_wc(1)
-            mean_of_plane(t)
+        means_of_planes([0, 1], "means01")
+        cast_wc(0)
+        cast_wc(1)
+        means_of_planes([2], "wc_raw1")
+        means_of_planes([3], "wc_raw1")
 
         wc_codes = keep.tile([P, N], U32, name="wc_codes", align_bytes=64)
         wc_scale = keep.tile([P, N], U8, name="wc_scale", align_bytes=64)
-        halve(fours_all[:], picked_all[:], 4)
-        nc.vector.quantize_mx(out=wc_codes[:].bitcast(FP8X4), scales=wc_scale[:], in_=wc_in[:])
-        halve(twos[0][:], fours[0], 2)
-        halve(twos[1][:], fours[1], 2)
-        finish_max(0)
-        halve(twos[2][:], fours[2], 2)
-        finish_max(1)
-        wb_scale = keep.tile([P, N], U8, name="wb_scale", tag="twos0", align_bytes=64)
-        deal(wb_scale[:], sb_raw)
-        halve(twos[3][:], fours[3], 2)
-        finish_max(2)
-        finish_max(3)
-
+        wb_scale = keep.tile([P, N], U8, name="wb_scale", tag="window3", align_bytes=64)
         u_codes = keep.tile([P, B], U32, name="u_codes", align_bytes=64)
         u_scale = keep.tile([P, B], U8, name="u_scale", align_bytes=64)
         v_codes = keep.tile([P, B], U32, name="v_codes", align_bytes=64)
         v_scale = keep.tile([P, B], U8, name="v_scale", align_bytes=64)
+        slots = picked_all[:].rearrange("p (t b h i) -> p b t h i", t=PACK, h=2, i=4)
+        nc.vector.tensor_tensor(
+            fours[:].rearrange("p (b t i) -> p b t i", t=PACK, i=4), slots[:, :, :, 0, :], slots[:, :, :, 1, :], MAX
+        )
+        nc.vector.quantize_mx(out=wc_codes[:].bitcast(FP8X4), scales=wc_scale[:], in_=wc_in[:])
+        halve(twos[:], fours[:], 2)
+        deal(wb_scale[:], sb_raw)
         nc.vector.quantize_mx(out=v_codes[:].bitcast(FP8X4), scales=v_scale[:], in_=v_in[:])
-        wa_codes = keep.tile([P, N], U32, name="wa_codes", tag="fours_all", align_bytes=64)
-        wa_scale = keep.tile([P, N], U8, name="wa_scale", tag="twos2", align_bytes=64)
+        halve(tops[:], twos[:], 1)
+        wa_codes = keep.tile([P, N], U32, name="wa_codes", tag="fours", align_bytes=64)
         deal(wa_codes[:].bitcast(I32), wa_raw[:].bitcast(I32))
+        nc.vector.tensor_tensor(
+            u_in[:].rearrange("p (b t) -> p b t", t=PACK),
+            tops[:].rearrange("p (b t) -> p b t", t=PACK),
+            fa_sb[:].unsqueeze(1).to_broadcast([P, B, PACK]),
+            MULT,
+        )
+        wa_scale = keep.tile([P, N], U8, name="wa_scale", tag="twos", align_bytes=64)
         deal(wa_scale[:], sa_raw)
         nc.vector.quantize_mx(out=u_codes[:].bitcast(FP8X4), scales=u_scale[:], in_=u_in[:])
 
@@ -183,8 +185,8 @@ def tile_list_group_range_pooling_pl_kernel(
 
         y_sb = keep.tile([P, PACK * B], F32, name="y_sb", align_bytes=64)
         y_rows = out_0.rearrange("(p s) b -> p (s b)", s=PACK)
-        nc.scalar.copy(out=y_sb[:, 0 : 2 * B], in_=banks[0][:].rearrange("p s b -> p (s b)"))
-        nc.vector.tensor_copy(out=y_sb[:, 2 * B : 4 * B], in_=banks[1][:].rearrange("p s b -> p (s b)"))
+        nc.vector.tensor_copy(out=y_sb[:, 0 : 2 * B], in_=banks[0][:].rearrange("p s b -> p (s b)"))
+        nc.scalar.copy(out=y_sb[:, 2 * B : 4 * B], in_=banks[1][:].rearrange("p s b -> p (s b)"))
         nc.sync.dma_start(out=y_rows[:, 0 : 2 * B], in_=y_sb[:, 0 : 2 * B])
         nc.sync.dma_start(out=y_rows[:, 2 * B : 4 * B], in_=y_sb[:, 2 * B : 4 * B])
 

@@ -15,7 +15,7 @@ U8 = mybir.dt.uint8
 FP8X4 = mybir.dt.float8_e4m3fn_x4
 FP4X4 = mybir.dt.float4_e2m1fn_x4
 MAX = mybir.AluOpType.max
-MULT = mybir.AluOpType.mult
+AXIS_X = mybir.AxisListType.X
 COPY = mybir.ActivationFunctionType.Copy
 
 P = 128
@@ -30,8 +30,8 @@ def tile_list_group_range_pooling_pl_kernel(
     nc = tc.nc
     with ExitStack() as ctx:
         keep = ctx.enter_context(tc.tile_pool(name="keep", bufs=1))
-        ps_sum = ctx.enter_context(tc.psum_pool(name="ps_sum", bufs=3))
-        ps_back = ctx.enter_context(tc.psum_pool(name="ps_back", bufs=3))
+        shared = ctx.enter_context(tc.tile_pool(name="shared", bufs=1))
+        ps_sum = ctx.enter_context(tc.psum_pool(name="ps_sum", bufs=1))
         ps_y = ctx.enter_context(tc.psum_pool(name="ps_y", bufs=1))
 
         offsets = keep.tile([P, J // 16], U16, name="offsets")
@@ -39,7 +39,10 @@ def tile_list_group_range_pooling_pl_kernel(
         x_planes = xt.rearrange("(p t) c -> t p c", t=PACK)
         wc_rows = wc.rearrange("(p j) n -> p j n", j=PACK)
         half = N // 2
-        wc_raw = [keep.tile([P, PACK, half], F32, name="wc_raw%d" % h, align_bytes=64) for h in range(2)]
+        wc_raw = [
+            keep.tile([P, PACK, half], F32, name="wc_raw0", align_bytes=64),
+            shared.tile([P, PACK, half], F32, name="wc_raw1", align_bytes=64, offset=0),
+        ]
         wa_raw = keep.tile([P, N], U32, name="wa_raw", align_bytes=64)
         wb_raw = keep.tile([P, 2 * N], U8, name="wb_raw", align_bytes=64)
         gq_codes = keep.tile([P, 2 * B], U8, name="gq_codes", align_bytes=64)
@@ -67,12 +70,12 @@ def tile_list_group_range_pooling_pl_kernel(
         nc.sync.dma_start(out=wc_raw[1][:], in_=wc_rows[:, :, half:N])
         nc.sync.dma_start(out=wa_raw[:].bitcast(I32), in_=wa_words[0].rearrange("p n r -> p (n r)").bitcast(I32))
         nc.sync.dma_start(out=gq_codes[:].bitcast(I32), in_=gq_words[0].bitcast(I32))
-        load_scale_rows(nc.sync, sa_raw, wa_scales)
+        load_scale_rows(nc.sync, gq_scale, gq_scales)
 
         ident = keep.tile([P, P], F32, name="ident", align_bytes=64)
         make_identity(nc, ident[:])
         load_scale_rows(nc.gpsimd, sb_raw, wb_scales)
-        load_scale_rows(nc.gpsimd, gq_scale, gq_scales)
+        load_scale_rows(nc.gpsimd, sa_raw, wa_scales)
 
         wb_codes = keep.tile([P, 2 * N], U8, name="wb_codes", align_bytes=64)
         nc.vector.tensor_copy(
@@ -81,15 +84,20 @@ def tile_list_group_range_pooling_pl_kernel(
         )
 
         def deal(dealt, raw):
-            nc.vector.tensor_copy(out=dealt.rearrange("p (s m) -> p m s", s=PACK), in_=raw.rearrange("p (m s) -> p m s", s=PACK))
+            nc.gpsimd.tensor_copy(out=dealt.rearrange("p (s m) -> p s m", s=PACK), in_=raw.rearrange("p (m s) -> p s m", s=PACK))
 
-        picked_all = keep.tile([P, PACK * J], F32, name="picked_all", align_bytes=64)
-        picked = [picked_all[:, t * J : (t + 1) * J] for t in range(PACK)]
-        u_in = keep.tile([P, B * PACK], BF16, name="u_in", align_bytes=64)
+        wa_codes = keep.tile([P, N], U32, name="wa_codes", align_bytes=64)
+        wa_scale = keep.tile([P, N], U8, name="wa_scale", align_bytes=64)
+        wb_scale = keep.tile([P, N], U8, name="wb_scale", align_bytes=64)
+        deal(wb_scale[:], sb_raw)
+        deal(wa_scale[:], sa_raw)
+        deal(wa_codes[:].bitcast(I32), wa_raw[:].bitcast(I32))
+
+        picked = [keep.tile([P, J], F32, name="picked%d" % t, align_bytes=64) for t in range(PACK)]
         v_in = keep.tile([P, B * PACK], BF16, name="v_in", align_bytes=64)
 
-        def means_of_planes(planes, tag):
-            sums = ps_sum.tile([P, len(planes) * P], F32, name="sums")
+        def means_of_planes(planes, means, bank):
+            sums = ps_sum.tile([P, len(planes) * P], F32, name="sums", tag=bank)
             for n, t in enumerate(planes):
                 for r in range(GROUP):
                     nc.tensor.matmul(
@@ -100,103 +108,111 @@ def tile_list_group_range_pooling_pl_kernel(
                         start=(r == 0),
                         stop=(r == GROUP - 1),
                     )
-            means = keep.tile([P, len(planes) * P], F32, name="means", tag=tag, align_bytes=64)
-            nc.scalar.activation(out=means[:], in_=sums[:], func=COPY, scale=1.0 / GROUP)
-            for n, t in enumerate(planes):
-                back = ps_back.tile([P, P], F32, name="back")
-                nc.tensor.transpose(back[:], means[:, n * P : (n + 1) * P], ident[:])
-                nc.scalar.activation(out=v_in[:, t : B * PACK : PACK], in_=back[:], func=COPY, scale=fb_sb[:, t : t + 1])
+            nc.scalar.activation(out=means, in_=sums[:], func=COPY, scale=1.0 / GROUP)
 
-        def halve(dst, src, width):
-            pairs = src.rearrange("p (g h i) -> p g h i", h=2, i=width)
-            nc.vector.tensor_tensor(dst.rearrange("p (g i) -> p g i", i=width), pairs[:, :, 0, :], pairs[:, :, 1, :], MAX)
-
-        fours = keep.tile([P, PACK * J // 2], F32, name="fours", align_bytes=64)
-        twos = keep.tile([P, PACK * J // 4], F32, name="twos", align_bytes=64)
-        tops = keep.tile([P, PACK * B], F32, name="tops", align_bytes=64)
+        def v_plane(t, means):
+            back = ps_sum.tile([P, P], F32, name="back", tag="turned%d" % t)
+            nc.tensor.transpose(back[:], means, ident[:])
+            nc.scalar.activation(out=v_in[:, t : B * PACK : PACK], in_=back[:], func=COPY, scale=fb_sb[:, t : t + 1])
 
         wc_in = keep.tile([P, N * PACK], BF16, name="wc_in", align_bytes=64)
-        wc_view = wc_in[:].rearrange("p (s m j) -> p m s j", s=PACK, j=PACK)
+        wc_view = wc_in[:].rearrange("p (s m j) -> p m j s", s=PACK, j=PACK)
 
         def cast_wc(h):
             ms = half // PACK
             nc.scalar.copy(
-                out=wc_view[:, h * ms : (h + 1) * ms, :, :], in_=wc_raw[h][:].rearrange("p j (m s) -> p m s j", s=PACK)
+                out=wc_view[:, h * ms : (h + 1) * ms, :, :], in_=wc_raw[h][:].rearrange("p j (m s) -> p m j s", s=PACK)
             )
 
         for t in range(PACK):
-            nc.vector.tensor_copy(picked[t], window[t][:].indirect(offsets[:]))
-        means_of_planes([0, 1], "means01")
+            nc.vector.tensor_copy(picked[t][:], window[t][:].indirect(offsets[:]))
+        means01 = keep.tile([P, 2 * P], F32, name="means01", align_bytes=64)
+        means_of_planes([0, 1], means01[:], "first")
+        v_plane(0, means01[:, 0:P])
+        v_plane(1, means01[:, P : 2 * P])
         cast_wc(0)
         cast_wc(1)
-        means_of_planes([2], "wc_raw1")
-        means_of_planes([3], "wc_raw1")
 
-        wc_codes = keep.tile([P, N], U32, name="wc_codes", align_bytes=64)
-        wc_scale = keep.tile([P, N], U8, name="wc_scale", align_bytes=64)
-        wb_scale = keep.tile([P, N], U8, name="wb_scale", tag="window3", align_bytes=64)
+        means2 = shared.tile([P, P], F32, name="means2", align_bytes=64, offset=0)
+        means3 = shared.tile([P, P], F32, name="means3", align_bytes=64, offset=4 * P)
+        u_in = shared.tile([P, B * PACK], BF16, name="u_in", align_bytes=64, offset=0)
+        tops = keep.tile([P, PACK * B], F32, name="tops", tag="window3", align_bytes=64)
+
+        def u_plane(t):
+            top = tops[:, t * B : (t + 1) * B]
+            nc.vector.tensor_reduce(top, picked[t][:].rearrange("p (b r) -> p b r", r=GROUP), AXIS_X, MAX)
+            nc.scalar.activation(out=u_in[:, t : B * PACK : PACK], in_=top, func=COPY, scale=fa_sb[:, t : t + 1])
+
+        means_of_planes([2], means2[:], "first")
+        means_of_planes([3], means3[:], "turned0")
+        v_plane(2, means2[:])
+        v_plane(3, means3[:])
+        wc_scale = [keep.tile([P, half], U8, name="wc_scale%d" % h, align_bytes=64) for h in range(2)]
+        wc_codes = []
+
+        def quantize_wc(h):
+            codes = keep.tile([P, half], U32, name="wc_codes%d" % h, tag="picked%d" % (h + 1), align_bytes=64)
+            nc.vector.quantize_mx(
+                out=codes[:].bitcast(FP8X4), scales=wc_scale[h][:], in_=wc_in[:, h * half * PACK : (h + 1) * half * PACK]
+            )
+            wc_codes.append(codes)
+
+        for t in range(PACK - 1):
+            u_plane(t)
+        quantize_wc(0)
+        u_plane(PACK - 1)
+
         u_codes = keep.tile([P, B], U32, name="u_codes", align_bytes=64)
         u_scale = keep.tile([P, B], U8, name="u_scale", align_bytes=64)
         v_codes = keep.tile([P, B], U32, name="v_codes", align_bytes=64)
         v_scale = keep.tile([P, B], U8, name="v_scale", align_bytes=64)
-        slots = picked_all[:].rearrange("p (t b h i) -> p b t h i", t=PACK, h=2, i=4)
-        nc.vector.tensor_tensor(
-            fours[:].rearrange("p (b t i) -> p b t i", t=PACK, i=4), slots[:, :, :, 0, :], slots[:, :, :, 1, :], MAX
-        )
-        nc.vector.quantize_mx(out=wc_codes[:].bitcast(FP8X4), scales=wc_scale[:], in_=wc_in[:])
-        halve(twos[:], fours[:], 2)
-        deal(wb_scale[:], sb_raw)
         nc.vector.quantize_mx(out=v_codes[:].bitcast(FP8X4), scales=v_scale[:], in_=v_in[:])
-        halve(tops[:], twos[:], 1)
-        wa_codes = keep.tile([P, N], U32, name="wa_codes", tag="fours", align_bytes=64)
-        deal(wa_codes[:].bitcast(I32), wa_raw[:].bitcast(I32))
-        nc.vector.tensor_tensor(
-            u_in[:].rearrange("p (b t) -> p b t", t=PACK),
-            tops[:].rearrange("p (b t) -> p b t", t=PACK),
-            fa_sb[:].unsqueeze(1).to_broadcast([P, B, PACK]),
-            MULT,
-        )
-        wa_scale = keep.tile([P, N], U8, name="wa_scale", tag="twos", align_bytes=64)
-        deal(wa_scale[:], sa_raw)
+        quantize_wc(1)
         nc.vector.quantize_mx(out=u_codes[:].bitcast(FP8X4), scales=u_scale[:], in_=u_in[:])
 
         banks = [ps_y.tile([P, 2, B], F32, name="y_bank%d" % h) for h in range(2)]
-        for term in range(3):
-            for s in range(PACK):
-                cols = slice(s * P, (s + 1) * P)
-                if term == 0:
-                    lhs, lhs_scale = wc_codes[:, cols].bitcast(FP8X4), wc_scale[:, cols]
-                    rhs, rhs_scale = gq_codes[:].bitcast(FP4X4), gq_scale
-                elif term == 1:
-                    lhs, lhs_scale = wb_codes[:, 2 * s * P : 2 * (s + 1) * P].bitcast(FP4X4), wb_scale[:, cols]
-                    rhs, rhs_scale = v_codes[:].bitcast(FP8X4), v_scale[:]
-                else:
-                    lhs, lhs_scale = wa_codes[:, cols].bitcast(FP8X4), wa_scale[:, cols]
-                    rhs, rhs_scale = u_codes[:].bitcast(FP8X4), u_scale[:]
-                nc.tensor.matmul_mx(
-                    out=banks[s // 2][:, s % 2, :],
-                    lhsT=lhs,
-                    lhsT_scale=lhs_scale,
-                    rhs=rhs,
-                    rhs_scale=rhs_scale,
-                    start=(term == 0 and s % 2 == 0),
-                    stop=(term == 2 and s % 2 == 1),
-                )
 
-        y_sb = keep.tile([P, PACK * B], F32, name="y_sb", align_bytes=64)
+        def product(term, s, start=False, stop=False):
+            cols = slice(s * P, (s + 1) * P)
+            if term == "wc":
+                part = slice((s % 2) * P, (s % 2 + 1) * P)
+                lhs, lhs_scale = wc_codes[s // 2][:, part].bitcast(FP8X4), wc_scale[s // 2][:, part]
+                rhs, rhs_scale = gq_codes[:].bitcast(FP4X4), gq_scale
+            elif term == "wb":
+                lhs, lhs_scale = wb_codes[:, 2 * s * P : 2 * (s + 1) * P].bitcast(FP4X4), wb_scale[:, cols]
+                rhs, rhs_scale = v_codes[:].bitcast(FP8X4), v_scale[:]
+            else:
+                lhs, lhs_scale = wa_codes[:, cols].bitcast(FP8X4), wa_scale[:, cols]
+                rhs, rhs_scale = u_codes[:].bitcast(FP8X4), u_scale[:]
+            nc.tensor.matmul_mx(
+                out=banks[s // 2][:, s % 2, :], lhsT=lhs, lhsT_scale=lhs_scale, rhs=rhs, rhs_scale=rhs_scale, start=start, stop=stop
+            )
+
+        product("wc", 0, start=True)
+        product("wc", 1)
+        product("wb", 0)
+        product("wb", 1)
+        product("wb", 2, start=True)
+        product("wb", 3)
+        product("wc", 2)
+        product("wc", 3)
+        product("wa", 0)
+        product("wa", 1, stop=True)
+        product("wa", 2)
+        product("wa", 3, stop=True)
+
+        y_sb = [keep.tile([P, 2 * B], F32, name="y_sb%d" % h, align_bytes=64) for h in range(2)]
         y_rows = out_0.rearrange("(p s) b -> p (s b)", s=PACK)
-        nc.vector.tensor_copy(out=y_sb[:, 0 : 2 * B], in_=banks[0][:].rearrange("p s b -> p (s b)"))
-        nc.scalar.copy(out=y_sb[:, 2 * B : 4 * B], in_=banks[1][:].rearrange("p s b -> p (s b)"))
-        nc.sync.dma_start(out=y_rows[:, 0 : 2 * B], in_=y_sb[:, 0 : 2 * B])
-        nc.sync.dma_start(out=y_rows[:, 2 * B : 4 * B], in_=y_sb[:, 2 * B : 4 * B])
-
         y_in = keep.tile([P, B * PACK], BF16, name="y_in", align_bytes=64)
         y_codes = keep.tile([P, B], U32, name="y_codes", align_bytes=64)
         y_scale = keep.tile([P, B], U8, name="y_scale", align_bytes=64)
-        nc.vector.tensor_copy(
-            out=y_in[:].rearrange("p (c i s) -> p c s i", i=4, s=PACK),
-            in_=y_sb[:].rearrange("p (s c i) -> p c s i", s=PACK, i=4),
-        )
+        y_words = y_in[:].rearrange("p (b s) -> p b s", s=PACK)
+        nc.vector.tensor_copy(out=y_sb[0][:], in_=banks[0][:].rearrange("p s b -> p (s b)"))
+        nc.sync.dma_start(out=y_rows[:, 0 : 2 * B], in_=y_sb[0][:])
+        nc.vector.tensor_copy(out=y_words[:, :, 0:2], in_=banks[0][:].rearrange("p s b -> p b s"))
+        nc.scalar.copy(out=y_words[:, :, 2:4], in_=banks[1][:].rearrange("p s b -> p b s"))
+        nc.scalar.copy(out=y_sb[1][:], in_=banks[1][:].rearrange("p s b -> p (s b)"))
+        nc.sync.dma_start(out=y_rows[:, 2 * B : 4 * B], in_=y_sb[1][:])
         nc.vector.quantize_mx(out=y_codes[:].bitcast(FP8X4), scales=y_scale[:], in_=y_in[:])
         nc.sync.dma_start(out=out_1[0].rearrange("p c r -> p (c r)").bitcast(I32), in_=y_codes[:].bitcast(I32))
         for q in range(QUADS):

from contextlib import ExitStack

import concourse.mybir as mybir
from concourse.masks import make_identity

K, T, J, B, L, N = 512, 2048, 1024, 128, 512, 512
FLOPS = 3 * 2 * K * N * B

F32 = mybir.dt.float32
BF16 = mybir.dt.bfloat16
I32 = mybir.dt.int32
U32 = mybir.dt.uint32
U16 = mybir.dt.uint16
U8 = mybir.dt.uint8
FP8X4 = mybir.dt.float8_e4m3fn_x4
FP4X4 = mybir.dt.float4_e2m1fn_x4
MAX = mybir.AluOpType.max
AXIS_X = mybir.AxisListType.X
COPY = mybir.ActivationFunctionType.Copy

P = 128
PACK = 4
GROUP = J // B
QUADS = 4


def tile_list_group_range_pooling_pl_kernel(
    tc, xt, fa, fb, wa_words, wa_scales, wb_words, wb_scales, gq_words, gq_scales, wc, offs, out_0, out_1, out_2
):
    nc = tc.nc
    with ExitStack() as ctx:
        keep = ctx.enter_context(tc.tile_pool(name="keep", bufs=1))
        shared = ctx.enter_context(tc.tile_pool(name="shared", bufs=1))
        ps_sum = ctx.enter_context(tc.psum_pool(name="ps_sum", bufs=1))
        ps_y = ctx.enter_context(tc.psum_pool(name="ps_y", bufs=1))

        offsets = keep.tile([P, J // 16], U16, name="offsets")
        window = [keep.tile([P, T], F32, name="window%d" % t, align_bytes=64) for t in range(PACK)]
        x_planes = xt.rearrange("(p t) c -> t p c", t=PACK)
        wc_rows = wc.rearrange("(p j) n -> p j n", j=PACK)
        half = N // 2
        wc_raw = [
            keep.tile([P, PACK, half], F32, name="wc_raw0", align_bytes=64),
            shared.tile([P, PACK, half], F32, name="wc_raw1", align_bytes=64, offset=0),
        ]
        wa_raw = keep.tile([P, N], U32, name="wa_raw", align_bytes=64)
        wb_raw = keep.tile([P, 2 * N], U8, name="wb_raw", align_bytes=64)
        gq_codes = keep.tile([P, 2 * B], U8, name="gq_codes", align_bytes=64)
        fa_sb = keep.tile([P, PACK], F32, name="fa_sb")
        fb_sb = keep.tile([P, PACK], F32, name="fb_sb")
        sb_tile = keep.tile([P, N], U8, name="sb_raw", align_bytes=64)
        given = keep.tile([P, N + B], U8, name="given_scales", align_bytes=64)
        sa_raw, sb_raw, gq_scale = given[:, 0:N], sb_tile[:], given[:, N : N + B]

        def load_scale_rows(queue, dst, src):
            for q in range(QUADS):
                queue.dma_start(out=dst[32 * q : 32 * q + 4, :].bitcast(I32), in_=src[0, 4 * q : 4 * q + 4, :].bitcast(I32))

        nc.vector.memset(sb_raw.bitcast(I32), 0)
        nc.vector.memset(given[:].bitcast(I32), 0)

        nc.sync.dma_start(offsets[:], offs)
        nc.sync.dma_start(out=window[0][:], in_=x_planes[0])
        nc.scalar.dma_start(out=wb_raw[:].bitcast(I32), in_=wb_words[0].bitcast(I32))
        nc.scalar.dma_start(out=fb_sb[:], in_=fb.rearrange("(p t) o -> p (t o)", t=PACK))
        nc.scalar.dma_start(out=fa_sb[:], in_=fa.rearrange("(p t) o -> p (t o)", t=PACK))
        for t in range(1, PACK):
            nc.sync.dma_start(out=window[t][:], in_=x_planes[t])
        nc.sync.dma_start(out=wc_raw[0][:], in_=wc_rows[:, :, 0:half])
        nc.sync.dma_start(out=wc_raw[1][:], in_=wc_rows[:, :, half:N])
        nc.sync.dma_start(out=wa_raw[:].bitcast(I32), in_=wa_words[0].rearrange("p n r -> p (n r)").bitcast(I32))
        nc.sync.dma_start(out=gq_codes[:].bitcast(I32), in_=gq_words[0].bitcast(I32))
        load_scale_rows(nc.sync, gq_scale, gq_scales)

        ident = keep.tile([P, P], F32, name="ident", align_bytes=64)
        make_identity(nc, ident[:])
        load_scale_rows(nc.gpsimd, sb_raw, wb_scales)
        load_scale_rows(nc.gpsimd, sa_raw, wa_scales)

        wb_codes = keep.tile([P, 2 * N], U8, name="wb_codes", align_bytes=64)
        nc.vector.tensor_copy(
            out=wb_codes[:].rearrange("p (s m e) -> p m s e", s=PACK, e=2),
            in_=wb_raw[:].rearrange("p (m s e) -> p m s e", s=PACK, e=2),
        )

        def deal(dealt, raw):
            nc.gpsimd.tensor_copy(out=dealt.rearrange("p (s m) -> p s m", s=PACK), in_=raw.rearrange("p (m s) -> p s m", s=PACK))

        wa_codes = keep.tile([P, N], U32, name="wa_codes", align_bytes=64)
        wa_scale = keep.tile([P, N], U8, name="wa_scale", align_bytes=64)
        wb_scale = keep.tile([P, N], U8, name="wb_scale", align_bytes=64)
        deal(wb_scale[:], sb_raw)
        deal(wa_scale[:], sa_raw)
        deal(wa_codes[:].bitcast(I32), wa_raw[:].bitcast(I32))

        picked = [keep.tile([P, J], F32, name="picked%d" % t, align_bytes=64) for t in range(PACK)]
        v_in = keep.tile([P, B * PACK], BF16, name="v_in", align_bytes=64)

        def means_of_planes(planes, means, bank):
            sums = ps_sum.tile([P, len(planes) * P], F32, name="sums", tag=bank)
            for n, t in enumerate(planes):
                for r in range(GROUP):
                    nc.tensor.matmul(
                        sums[:, n * P : (n + 1) * P],
                        lhsT=picked[t][:, r:J:GROUP],
                        rhs=ident[:],
                        is_transpose=True,
                        start=(r == 0),
                        stop=(r == GROUP - 1),
                    )
            nc.scalar.activation(out=means, in_=sums[:], func=COPY, scale=1.0 / GROUP)

        def v_plane(t, means):
            back = ps_sum.tile([P, P], F32, name="back", tag="turned%d" % t)
            nc.tensor.transpose(back[:], means, ident[:])
            nc.scalar.activation(out=v_in[:, t : B * PACK : PACK], in_=back[:], func=COPY, scale=fb_sb[:, t : t + 1])

        wc_in = keep.tile([P, N * PACK], BF16, name="wc_in", align_bytes=64)
        wc_view = wc_in[:].rearrange("p (s m j) -> p m j s", s=PACK, j=PACK)

        def cast_wc(h):
            ms = half // PACK
            nc.scalar.copy(
                out=wc_view[:, h * ms : (h + 1) * ms, :, :], in_=wc_raw[h][:].rearrange("p j (m s) -> p m j s", s=PACK)
            )

        for t in range(PACK):
            nc.vector.tensor_copy(picked[t][:], window[t][:].indirect(offsets[:]))
        means01 = keep.tile([P, 2 * P], F32, name="means01", align_bytes=64)
        means_of_planes([0, 1], means01[:], "first")
        v_plane(0, means01[:, 0:P])
        v_plane(1, means01[:, P : 2 * P])
        cast_wc(0)
        cast_wc(1)

        means2 = shared.tile([P, P], F32, name="means2", align_bytes=64, offset=0)
        means3 = shared.tile([P, P], F32, name="means3", align_bytes=64, offset=4 * P)
        u_in = shared.tile([P, B * PACK], BF16, name="u_in", align_bytes=64, offset=0)
        tops = keep.tile([P, PACK * B], F32, name="tops", tag="window3", align_bytes=64)

        def u_plane(t):
            top = tops[:, t * B : (t + 1) * B]
            nc.vector.tensor_reduce(top, picked[t][:].rearrange("p (b r) -> p b r", r=GROUP), AXIS_X, MAX)
            nc.scalar.activation(out=u_in[:, t : B * PACK : PACK], in_=top, func=COPY, scale=fa_sb[:, t : t + 1])

        means_of_planes([2], means2[:], "first")
        means_of_planes([3], means3[:], "turned0")
        v_plane(2, means2[:])
        v_plane(3, means3[:])
        wc_scale = [keep.tile([P, half], U8, name="wc_scale%d" % h, align_bytes=64) for h in range(2)]
        wc_codes = []

        def quantize_wc(h):
            codes = keep.tile([P, half], U32, name="wc_codes%d" % h, tag="picked%d" % (h + 1), align_bytes=64)
            nc.vector.quantize_mx(
                out=codes[:].bitcast(FP8X4), scales=wc_scale[h][:], in_=wc_in[:, h * half * PACK : (h + 1) * half * PACK]
            )
            wc_codes.append(codes)

        for t in range(PACK - 1):
            u_plane(t)
        quantize_wc(0)
        u_plane(PACK - 1)

        u_codes = keep.tile([P, B], U32, name="u_codes", align_bytes=64)
        u_scale = keep.tile([P, B], U8, name="u_scale", align_bytes=64)
        v_codes = keep.tile([P, B], U32, name="v_codes", align_bytes=64)
        v_scale = keep.tile([P, B], U8, name="v_scale", align_bytes=64)
        nc.vector.quantize_mx(out=v_codes[:].bitcast(FP8X4), scales=v_scale[:], in_=v_in[:])
        quantize_wc(1)
        nc.vector.quantize_mx(out=u_codes[:].bitcast(FP8X4), scales=u_scale[:], in_=u_in[:])

        banks = [ps_y.tile([P, 2, B], F32, name="y_bank%d" % h) for h in range(2)]

        def product(term, s, start=False, stop=False):
            cols = slice(s * P, (s + 1) * P)
            if term == "wc":
                part = slice((s % 2) * P, (s % 2 + 1) * P)
                lhs, lhs_scale = wc_codes[s // 2][:, part].bitcast(FP8X4), wc_scale[s // 2][:, part]
                rhs, rhs_scale = gq_codes[:].bitcast(FP4X4), gq_scale
            elif term == "wb":
                lhs, lhs_scale = wb_codes[:, 2 * s * P : 2 * (s + 1) * P].bitcast(FP4X4), wb_scale[:, cols]
                rhs, rhs_scale = v_codes[:].bitcast(FP8X4), v_scale[:]
            else:
                lhs, lhs_scale = wa_codes[:, cols].bitcast(FP8X4), wa_scale[:, cols]
                rhs, rhs_scale = u_codes[:].bitcast(FP8X4), u_scale[:]
            nc.tensor.matmul_mx(
                out=banks[s // 2][:, s % 2, :], lhsT=lhs, lhsT_scale=lhs_scale, rhs=rhs, rhs_scale=rhs_scale, start=start, stop=stop
            )

        product("wc", 0, start=True)
        product("wc", 1)
        product("wb", 0)
        product("wb", 1)
        product("wb", 2, start=True)
        product("wb", 3)
        product("wc", 2)
        product("wc", 3)
        product("wa", 0)
        product("wa", 1, stop=True)
        product("wa", 2)
        product("wa", 3, stop=True)

        y_sb = [keep.tile([P, 2 * B], F32, name="y_sb%d" % h, align_bytes=64) for h in range(2)]
        y_rows = out_0.rearrange("(p s) b -> p (s b)", s=PACK)
        y_in = keep.tile([P, B * PACK], BF16, name="y_in", align_bytes=64)
        y_codes = keep.tile([P, B], U32, name="y_codes", align_bytes=64)
        y_scale = keep.tile([P, B], U8, name="y_scale", align_bytes=64)
        y_words = y_in[:].rearrange("p (b s) -> p b s", s=PACK)
        nc.vector.tensor_copy(out=y_sb[0][:], in_=banks[0][:].rearrange("p s b -> p (s b)"))
        nc.sync.dma_start(out=y_rows[:, 0 : 2 * B], in_=y_sb[0][:])
        nc.vector.tensor_copy(out=y_words[:, :, 0:2], in_=banks[0][:].rearrange("p s b -> p b s"))
        nc.scalar.copy(out=y_words[:, :, 2:4], in_=banks[1][:].rearrange("p s b -> p b s"))
        nc.scalar.copy(out=y_sb[1][:], in_=banks[1][:].rearrange("p s b -> p (s b)"))
        nc.sync.dma_start(out=y_rows[:, 2 * B : 4 * B], in_=y_sb[1][:])
        nc.vector.quantize_mx(out=y_codes[:].bitcast(FP8X4), scales=y_scale[:], in_=y_in[:])
        nc.sync.dma_start(out=out_1[0].rearrange("p c r -> p (c r)").bitcast(I32), in_=y_codes[:].bitcast(I32))
        for q in range(QUADS):
            queue = nc.scalar if q % 2 == 0 else nc.sync
            queue.dma_start(out=out_2[0, 4 * q : 4 * q + 4, :].bitcast(I32), in_=y_scale[32 * q : 32 * q + 4, :].bitcast(I32))
